import numpy as np, ml_dtypes
CORES = [2,3,42,43,82,83,122,123]
N = 8
import mx_ref
BF = ml_dtypes.bfloat16
def gcols(t, e):
    v = np.concatenate([t.reshape(8, 16, -1, 4), np.zeros((8, 16, 1, 4), BF)], axis=2)
    return np.ascontiguousarray(np.stack([v[g][:, e[g]] for g in range(8)])).reshape(128, -1)
def tile(rs):
    return np.stack(rs, axis=2).reshape(128, -1).astype(BF)
def cut(t, i, w=512):
    return t[:, w * i:w * i + w]
def gentries(a):
    return np.ascontiguousarray(a.reshape(8, 16, -1).transpose(0, 2, 1)).reshape(8, -1)
def gtable(e):
    e = np.asarray(e); return np.ascontiguousarray(e.reshape(8, -1, 16).transpose(0, 2, 1)).reshape(128, -1).astype(np.int32)
def pick(q, e):
    c = np.concatenate([q[0].reshape(128, -1, 4), np.zeros((128, 1, 4), np.uint8)], axis=1); s = np.concatenate([q[1], np.ones((16, 1), np.uint8)], axis=1)
    return (np.ascontiguousarray(c[:, e].reshape(128, -1)), np.ascontiguousarray(s[:, e]))
def join(*qs):
    return (np.concatenate([q[0] for q in qs], axis=1), np.concatenate([q[1] for q in qs], axis=1))
def put(q, e, v):
    c, s = q[0].reshape(128, -1, 4).copy(), q[1].copy(); c[:, e] = v[0].reshape(128, -1, 4); s[:, e] = v[1]
    return (c.reshape(128, -1), s)
def pk(c, s):
    return (np.ascontiguousarray(c), mx_ref.live(s))
def emit(q):
    return q[0], q[1]
def packed(v, rng):
    q = [mx_ref.quantize(np.ascontiguousarray(v[r])) for r in range(N)]
    return np.stack([a for a, b in q]), np.stack([mx_ref.plane(b, rng) for a, b in q])
def values_of_codes():
    e, c = np.zeros((128, 128, 4), np.float32), np.zeros((128, 2, 4), np.uint8)
    e[np.arange(128), np.arange(128), 0] = 1
    c[:127, :, 0] = np.arange(256).reshape(2, 128).T[:127]
    return mx_ref.matmul(mx_ref.quantize(e.reshape(128, 512).astype(BF)), (c.reshape(128, 8), np.full((16, 2), 127, np.uint8))).T.reshape(-1).astype(np.float64)
CODE_VALUE, SCALE_VALUE = values_of_codes(), 2.0 ** (np.arange(256) - 127.0)
def decode(q):
    return (CODE_VALUE[q[0]].reshape(16, 8, -1, 4) * SCALE_VALUE[q[1]][:, None, :, None] + 0.0).reshape(128, -1).astype(np.float32)
def f(rng, *shape):
    return mx_ref.flush((rng.standard_normal(shape, dtype=np.float32) * np.exp2(rng.integers(-2, 3, shape[:-1] + (1,)))).astype(BF))
def wide(rng, *shape, cols=0):
    v = rng.standard_normal(shape, dtype=np.float32) * np.exp2(rng.integers(-12, 13, shape)).astype(np.float32)
    if cols: v *= np.repeat(np.exp2(rng.integers(-cols, cols + 1, shape[:-2] + (1, shape[-1] // 4))) * (rng.random(shape[:-2] + (1, shape[-1] // 4)) > 0.0625), 4, axis=-1).astype(np.float32)
    return mx_ref.flush(v.astype(BF))
C, B, R = 256, 64, 3
def order(p):
    return np.argsort(-(p[::16] + np.float32(0.0)), axis=1, kind="stable")
def big(v):
    v = v.astype(np.float32)
    v[np.abs(v) < np.float32(2.0 ** -16)] = 0
    return v.astype(BF)
def numbers_of(rng):
    return {"x": big(f(rng, N, 128, 16 * C)), "u": np.array(f(rng, N, 128, 512)), "v": np.array(f(rng, N, 128, 512))}
def weights(rng, kept=[]):
    w = np.array(f(rng, N, 128, 2048)).reshape(N, 8, 16, 4, 8, 16, 4)
    for i in kept:
        w[:, :, i] = 0
        w[:, :, :, :, :, i] = 0
        for g in range(8):
            for k in range(4): w[:, g, i, k, g, i, k] = 32
    c, p = packed(w.reshape(N, 128, 2048), rng)
    return {"wc": c, "ws": p}
def paths(rng):
    a = np.zeros((N, 8, C), int)
    for r in range(N):
        for g in range(8):
            a[r, g, ::2] = rng.permutation(C // 2) * 2 + 1
            a[r, g, 1::2] = rng.permutation(C // 2) * 2
    return [a, rng.integers(0, B, (N, 8, C)), rng.integers(0, 4, (N, 8, C)), rng.integers(0, 4, (N, 8, C))]
def stored(p):
    return {k: np.stack([gtable(e[r]) for r in range(N)]) for k, e in zip(("la", "lb", "da", "db"), p)}
def plant(rng, p, z):
    x = np.zeros((N, 8, 16, 4, C, 4), np.float32)
    at = np.zeros((N, 8, C), int)
    for r in range(N):
        for g in range(8):
            a = p[0][r, g]
            at[r, g, a] = p[2][r, g]
            x[r, g][:, :, a] = z[r, g][:, None]
            x[r, g][:, :, :B][:, np.arange(4)[:, None] != at[r, g, :B]] = 0
    for r in range(N): p[3][r] = (np.take_along_axis(at[r - 1], p[1][r], axis=1) + rng.integers(1, 4, (8, C))) % 4
    return x.reshape(N, 128, 16 * C).astype(BF)
def signs(rng):
    return np.stack([rng.permutation(8) % 2 * 2.0 - 1.0 for r in range(N)])
def setup_inputs(rng):
    return {**numbers_of(rng), **weights(rng), **stored(paths(rng))}
def setup_inputs_ties(rng):
    d = numbers_of(rng)
    e = rng.permutation(N)
    x = d["x"].reshape(N, 8, 16, 4, C, 4)
    for r in range(N):
        k = np.zeros((4, C), int) if r == e[0] else rng.integers(0, 3, (4, C))
        a = x[r][:, :8, 0, :3].copy()
        a[:, :, 2] = 0
        x[r][:, :8] = a[:, :, k]
    x[e[1]] = 0
    u = d["u"].reshape(N, 8, 16, 8, 16, 4)
    k = u.copy()
    u[:, :, :, :, :2] = 0
    for g in range(8): u[:, g, :8, g, :2] = k[:, g, :8, g, :2]
    return {"x": x.reshape(N, 128, 16 * C), "u": u.reshape(N, 128, 512), "v": d["v"], **weights(rng, range(8)), **stored(paths(rng))}
def setup_inputs_near(rng):
    d = numbers_of(rng)
    p = paths(rng)
    z = np.zeros((N, 8, 16, C, 4), np.float32)
    u = d["u"].reshape(N, 128, 128, 4)
    u[:, :, ::16] = 0
    u[:, :, 1::16] = 0
    o, c = rng.permutation(N) % 4, signs(rng)
    upper = np.arange(C) // (C // 2)
    for r in range(N):
        i = (np.arange(C) + rng.integers(0, C, (8, 1))) % C
        if o[r] == 3: i = i % (C // 2) * 2 + upper
        s = (i + 1) // 2
        size = 1.0 if o[r] < 2 else 2.0 ** -4
        m = ((s[:, :, None] >> np.arange(8)) & 1) * np.exp2(np.arange(8) - 22.0) * size
        if o[r] < 2:
            z[r, :, 0, :, 0] = 2 * c[r][:, None]
            for g in rng.permutation(8)[:4]: z[r, g, 0, rng.integers(C), 0] *= np.float32(2.0 ** 29)
        if o[r] == 3: z[r, :, 0, :, 0] = (8 + upper) * 2.0 ** -29
        z[r, :, 1, :, 0] = rng.integers(-1, 2, (8, C)) * (2.0 if o[r] < 2 else 2.0 ** -26)
        z[r, :, 8] = m[:, :, :4]
        z[r, :, 9] = m[:, :, 4:]
        z[r, :, 10:] = rng.integers(4, 8, (8, 6, C, 4)) * 2.0 ** -19 * size
        k = 1.0 if o[r] == 0 else 2.0 ** -30
        for h in range(0, 128, 16):
            u[r, h, h, 0] = k
            u[r, h + 8:h + 10, h] = k
            u[r, h + 1, h + 1, 0] = k
    x = plant(rng, p, z)
    return {"x": x, "u": u.reshape(N, 128, 512), "v": d["v"], **weights(rng, range(16)), **stored(p)}
def setup_inputs_lags(rng):
    d = numbers_of(rng)
    p = paths(rng)
    p[2] = rng.integers(1, 3, (N, 8, C))
    x = d["x"].astype(np.float32).reshape(N, 8, 16, 4, C, 4)
    u = d["u"].reshape(N, 128, 128, 4)
    u[:, :, 1::16] = 0
    kind = rng.permutation(8)
    ends = [(3, 3), (0, 0), (9, 9), (9, 9), (9, 0), (9, 3), (3, 9), (9, 9)]
    for g in range(8):
        k = kind[g]
        x[:, g, 0, :, :, 0] = rng.integers(4, 8, (N, 4, C)) * 0.25 * [1, -1, 1, -1, 1, -1, 1, 0][k]
        u[:, 16 * g, 16 * g + 1, 0] = 1
        for i in range(2):
            if ends[k][i] < 9: p[2][:, g, i::2] = ends[k][i]
        if k == 2: p[0][:, g] = np.arange(C) ^ 1
        if k == 3: p[0][:, g] = (np.arange(C) + 1) % C
        if k == 4: p[1][:, g], p[3][:, g] = rng.integers(B), 0
        if k == 5: p[3][:, g] = 3
    return {"x": x.reshape(N, 128, 16 * C).astype(BF), "u": u.reshape(N, 128, 512), "v": d["v"], **weights(rng, [0]), **stored(p)}
def setup_inputs_huge(rng):
    d = numbers_of(rng)
    p = paths(rng)
    c = np.stack([rng.permutation(C) % 2 * 2.0 - 1.0 for r in range(N)])
    c[rng.permutation(N) < N // 2] = -1
    z = 2.0 ** 30 * (0.8 + 0.2 * rng.random((N, 8, 16, C, 4))) * c[:, None, None, :, None]
    x = plant(rng, p, z.astype(np.float32))
    u = d["u"].reshape(N, 128, 8, 16, 4)
    a = 2.0 ** 30 * (1 - 0.1 * rng.random((N, 128, 8, 2, 4))) * np.stack([signs(rng), signs(rng)], axis=2)[:, None, :, :, None]
    u[:, :, :, :2] = a.astype(np.float32).astype(BF)
    return {"x": x, "u": u.reshape(N, 128, 512), "v": d["v"], **weights(rng, range(16)), **stored(p)}
def setup_inputs_spread(rng):
    d = setup_inputs(rng)
    d["x"] = big(wide(rng, N, 128, 16 * C, cols=6))
    return d
def check_inputs(d):
    b = []
    for k in ("x", "u", "v"):
        a = np.abs(d[k].astype(np.float32))
        if not (np.isfinite(a).all() and ((a == 0) | (a >= 2.0 ** -30) & (a <= 2.0 ** 30)).all()): b.append("a value of " + k)
    none, least, most = [emit(mx_ref.quantize(np.full((128, 16), k, np.float32).astype(BF)))[1][0, 0] for k in (0.0, 2.0 ** -30, 2.0 ** 30)]
    for r in range(N):
        if ((d["wc"][r] == 0x7F) | (d["wc"][r] == 0xFF)).any(): b.append("wc: a code that is no number")
        s = mx_ref.live(d["ws"][r])
        if ((s != none) & ((s < least) | (s > most))).any(): b.append("ws: a scale out of range")
        a = gentries(d["la"][r])
        if (np.sort(a, axis=1) != np.arange(C)).any(): b.append("la: no permutation")
        if ((a + np.arange(C)) % 2 != 1).any(): b.append("la: a number of the same parity")
        for k, n in (("lb", B), ("da", 4), ("db", 4)):
            if ((d[k][r] < 0) | (d[k][r] >= n)).any(): b.append(k + " out of range")
    return b
def reference(x, u, v, wc, ws, la, lb, da, db):
    qu = [mx_ref.quantize(u[r]) for r in range(N)]
    lay = [pk(wc[r], ws[r]) for r in range(N)]
    ring = [x[r] for r in range(N)]
    came = decode(join(*[mx_ref.quantize(np.ascontiguousarray(x[r].reshape(128, 4, C, 4)[:, :, :B]).reshape(128, -1)) for r in range(N)])).astype(BF)
    edge = [cut(came, (r - 1) % N, 16 * B) for r in range(N)]
    lag = np.zeros((N, 8, C), np.int64)
    last = [None] * N
    for t in range(R):
        sent = []
        for r in range(N):
            a = gentries(la[r])
            delay = gentries(da[r]) + lag[r] - np.take_along_axis(lag[r], a, axis=1)
            own = gcols(ring[r], C * delay + a)
            far = gcols(edge[r], B * gentries(db[r]) + gentries(lb[r]))
            q = mx_ref.quantize(((own.astype(np.float32) + far.astype(np.float32)) * np.float32(0.5)).astype(BF))
            s = mx_ref.matmul(qu[r], q)
            h = tile([mx_ref.matmul(pick(lay[r], np.arange(128 * b, 128 * b + 128)), q) * np.float32(0.03125) for b in range(4)])
            last[r] = h
            ring[r] = np.concatenate([h, ring[r][:, :12 * C]], axis=1)
            sent.append(mx_ref.quantize(gcols(h, order(s)[:, :B])))
            step = ((s[1::16] > 0).astype(np.int64) - (s[1::16] < 0)) * (np.arange(C) % 2 == t % 2)
            one = delay + step
            two = np.take_along_axis(delay, np.argsort(a, axis=1), axis=1) - step
            lag[r] += np.where((one >= 0) & (one <= 3) & (two >= 0) & (two <= 3), step, 0)
        if t < R - 1:
            came = decode(join(*sent)).astype(BF)
            edge = [np.concatenate([cut(came, (r - 1) % N, 4 * B), edge[r][:, :12 * B]], axis=1) for r in range(N)]
    y, ol = np.zeros((N, 128, C), np.float32), np.zeros((N, 8, C), np.float32)
    oc, osc = np.zeros((N, 128, 4 * C), np.uint8), np.zeros((N, 16, C), np.uint8)
    for r in range(N):
        q = mx_ref.quantize(last[r])
        y[r] = mx_ref.matmul(mx_ref.quantize(v[r]), q)
        ol[r] = lag[r]
        oc[r], osc[r] = emit(q)
    return {"y": y, "ol": ol, "oc": oc, "osc": osc}

@@ -1,0 +1,423 @@
+from concourse.mybir import dt, AluOpType, AxisListType, ActivationFunctionType
+
+C = 256
+BIG = 2.0 ** 96
+DIRECT = [5, 6, 7, 8, 9]
+SIGNED = [c for c in range(16) if c not in DIRECT]
+
+X4, U8, BF, F32, I32, U16 = "float8_e4m3fn_x4", "uint8", "bfloat16", "float32", "int32", "uint16"
+SCRATCH = {"ps": ("psum", [128, 4096], F32)}
+for _d, _names in (
+        (X4, "wq:512 uq:128 uq2:256 vq:128 eq:512 gq:128 zq:256 mq:1280 sq0:256 sq1:256 sq2:256 sq3:256 lq0:256 lq1:256 lq2:256"),
+        (U8, "wsc:512 us:128 us2:256 vs:128 es:512 gs:128 zs:256 ms:1280 ss0:256 ss1:256 ss2:256 ss3:256 ls0:256 ls1:256 ls2:256"),
+        (U16, "eo1:4 eo2:4 el1:4 el2:4 ulu:16 ownu:64 faru:48 au:16 fu:16 cu:16 llu:64 endu:4"),
+        (I32, "ia:16 ib:16 if_:16 im:16 pi:4 bi:32"),
+        (BF, "ring:7168 xb:1024 ub:512 vb:512 ones:514 c0:514 c1:514 g8:512 gt:512 y16:256 m0:256 mask2:256 reset:256 keep:256 tb:16 "
+             "wv:256 fr:256 e0:256 er0:256 e1:256 er1:256 e2:256 er2:256 hi:128 lo:128 mx:128 mn:128 sg:128 tm:128 d2:128 ym:256 ys:256 "
+             "own:1024 z:1024 dpl:1024 bord:1536 mt:5120"),
+        (F32, "pf:8 jf:256 nb:8 node2:32 t1:16 t2:16 t3:16 off0:64 off1:64 off2:64 o0:16 dp:16 t5:16 mk:32 mk2:32 mk3:32 t64:16 ac:32 xx:32 "
+              "t0:32 ll:64 lf:256 d1:256 sc:256 key:256 junk:768 junkv:512 ff:8 fd:4 fe:4 yo:256")):
+    for _e in _names.split():
+        SCRATCH[_e.split(":")[0]] = ("sbuf", [128, int(_e.split(":")[1])], _d)
+SEMAPHORES = ["cv", "cs", "ct", "cg", "sent", "arr0", "arr1", "arr2", "lst1", "lst2",
+              "dxb", "dx", "du", "dv", "dw", "dla", "dlb", "dda", "ddb", "dout"]
+
+A = AluOpType
+ACT = ActivationFunctionType
+
+
+def rank_program(g, core, T, topo):
+    rank = T.rank_of(core)
+    if rank is None:
+        return
+    n = len(T.cores)
+    nxt = T.cores[(rank + 1) % n]
+    prv = T.cores[(rank - 1) % n]
+    rid, pid, _ = topo.addr(nxt)
+    out_eng = topo.engines(core, nxt)[:8]
+    mask = sum(1 << e for e in out_eng)
+    n_in = len(topo.engines(prv, core)[:8])
+
+    Q = {"g": g, "v": g.vector, "s": g.scalar, "t": g.tensor, "y": g.sync}
+    csem = {"g": "cg", "v": "cv", "s": "cs", "t": "ct"}
+    total, snap, writer, readers, waited = {}, {}, {}, {}, {}
+    known = {q: {} for q in Q}
+
+    def wait(q, ev):
+        s, v = ev
+        if known[q].get(s, 0) >= v:
+            return
+        Q[q].wait_ge(T.sem[s], v)
+        waited[s] = max(waited.get(s, 0), v)
+        known[q][s] = v
+        for k, w in snap.get(ev, {}).items():
+            if known[q].get(k, 0) < w:
+                known[q][k] = w
+
+    def deps(q, reads, writes):
+        need = []
+        for r in reads:
+            if r in writer:
+                need.append(writer[r])
+            if r.startswith("ps"):
+                need += [e for e in readers.get(r, []) if e[0] != csem.get(q)]
+        for w in writes:
+            if w in writer:
+                need.append(writer[w])
+            need += readers.get(w, [])
+        if q == "t":
+            need = [e for e in need if e[0] != "ct"]
+        best = {}
+        for s, v in need:
+            best[s] = max(best.get(s, 0), v)
+        for s in sorted(best, key=lambda k: -len(snap.get((k, best[k]), {}))):
+            wait(q, (s, best[s]))
+
+    def done(ev, q, reads, writes):
+        new = dict(known[q])
+        for k, w in snap.get(ev, {}).items():
+            new[k] = max(new.get(k, 0), w)
+        snap[ev] = new
+        for r in reads:
+            readers.setdefault(r, []).append(ev)
+        for w in writes:
+            writer[w] = ev
+            readers[w] = []
+
+    def op(q, fn, reads, writes):
+        reads, writes = reads.split(), writes.split()
+        deps(q, reads, writes)
+        s = csem[q]
+        total[s] = total.get(s, 0) + 1
+        fn().then_inc(T.sem[s], 1)
+        done((s, total[s]), q, reads, writes)
+
+    def dma(q, sem, whole, out, in_, reads, writes):
+        reads, writes = reads.split(), writes.split()
+        deps(q, reads, [])
+        Q[q].dma_start(out, in_).then_inc(T.sem[sem], 16)
+        total[sem] = whole
+        done((sem, whole), q, reads, writes)
+
+    def send(out, in_, sem, reads):
+        deps("g", reads.split(), [])
+        g.remote_dma(out, in_, T.sem[sem], T.sem.sent, pid, rid, mask)
+        total["sent"] = total.get("sent", 0) + len(out_eng)
+
+    V, S, P = g.vector, g.scalar, g.tensor
+
+    def ts(out, in0, s1, o0, reads, writes, s2=None, o1=None):
+        if o1 is None:
+            op("v", lambda: V.tensor_scalar(out, in0, s1, None, o0), reads, writes)
+        else:
+            op("v", lambda: V.tensor_scalar(out, in0, s1, s2, o0, o1), reads, writes)
+
+    def tt(out, a, b, o, reads, writes):
+        op("v", lambda: V.tensor_tensor(out, a, b, o), reads, writes)
+
+    def cp(out, a, reads, writes):
+        op("v", lambda: V.tensor_copy(out, a), reads, writes)
+
+    def qz(q, s, a, reads, writes):
+        op("v", lambda: V.quantize_mx(q, s, a), reads, writes)
+
+    def scan(out, d0, d1, o0, o1, reads, writes):
+        op("v", lambda: V.tensor_tensor_scan(out, d0, d1, 0.0, o0, o1), reads, writes)
+
+    def act(out, a, f, reads, writes, **kw):
+        op("s", lambda: S.activation(out, a, f, **kw), reads, writes)
+
+    def bank(k, w=C):
+        return T.ps[:, 512 * k:512 * k + w]
+
+    def pair(q, s, a, b):
+        return T[q][:, a:b], T[s][:, a:b]
+
+    def mm(k, l, r, reads, start=True, stop=True, w=C):
+        op("t", lambda: P.matmul_mx(bank(k, w), l[0], l[1], r[0], r[1], start, stop), reads, "ps%d" % k)
+
+    def scaled(q, out, k, f, name, w=C):
+        if q == "v":
+            ts(out, bank(k, w), f, A.mult, "ps%d" % k, name)
+        else:
+            act(out, bank(k, w), ACT.Copy, "ps%d" % k, name, scale=f)
+
+    def iota(out, pattern, base, cm, name):
+        op("g", lambda: g.iota(out, pattern, base, cm, allow_small_or_imprecise_dtypes=True), "", name)
+
+    def u8(b):
+        return b.bitcast(dt.uint8)
+
+    def four(s):
+        return " ".join(s % b for b in range(4))
+
+    for s, k, w in (("arr0", 2, "l0"), ("arr1", 2, "l1"), ("arr2", 2, "l2"), ("lst1", 1, "el1"), ("lst2", 1, "el2")):
+        total[s] = k * n_in
+        writer[w] = (s, k * n_in)
+
+    for k in range(4):
+        dma("y" if k < 2 else "s", "dxb", 64, T.xb[:, 256 * k:256 * k + 256], T.x[:, 1024 * k:1024 * k + 256], "", "xb")
+    dma("s", "dla", 16, T.ia[:], T.la[:], "", "ia")
+    dma("s", "dda", 16, T.if_[:], T.da[:], "", "if")
+    dma("s", "dlb", 16, T.ib[:], T.lb[:], "", "ib")
+    dma("s", "ddb", 16, T.im[:], T.db[:], "", "im")
+    dma("y", "du", 16, T.ub[:], T.u[:], "", "ub")
+    for k in range(4):
+        dma("y", "dx", 64, T.ring[:, 3072 + 1024 * k + 256:4096 + 1024 * k], T.x[:, 1024 * k + 256:1024 * k + 1024], "", "ringx")
+    for k in range(4):
+        act(T.ring[:, 3072 + 1024 * k:3072 + 1024 * k + 256], T.xb[:, 256 * k:256 * k + 256], ACT.Copy, "xb", "rx%d" % k)
+
+    op("v", lambda: V.memset(T.ones[:], 1.0), "", "ones")
+    op("g", lambda: g.iota(T.pi[:, 3:4], [[1, 1]], 0, 1), "", "pi3")
+    iota(T.y16[:], [[0, 16], [1, 16]], 0, 0, "y16")
+    iota(T.jf[:], [[1, 256]], 0, 0, "jf")
+    op("g", lambda: g.affine_select(T.c0[:], T.ones[:], [[1, 514]], A.is_equal, 0.0, -2, -4), "ones", "c0")
+    op("v", lambda: V.memset(T.lf[:], 0.0), "", "lf")
+    ts(T.pi[:, 0:1], T.pi[:, 3:4], 15, A.bitwise_and, "pi3", "pi0")
+    ts(T.pi[:, 1:2], T.pi[:, 3:4], 4, A.logical_shift_right, "pi3", "pi1")
+    ts(T.pi[:, 2:3], T.pi[:, 3:4], 1, A.bitwise_and, "pi3", "pi2")
+    ts(T.reset[:], T.y16[:], 0.0, A.is_equal, "y16", "reset", BIG, A.mult)
+    cp(T.pf[:, 0:3], T.pi[:, 0:3], "pi0 pi1 pi2", "pf")
+    ts(T.keep[:], T.y16[:], 0.0, A.not_equal, "y16", "keep")
+    R_, G_, PAR, R4, S1024, SINV, PAR4, R16 = [T.pf[:, k:k + 1] for k in range(8)]
+    ts(R4, R_, 4.0, A.mult, "pf", "r4")
+    ts(S1024, PAR, -2048.0, A.mult, "pf", "s1024", 1024.0, A.add)
+    ts(SINV, PAR, -2.0 / 1024, A.mult, "pf", "sinv", 1.0 / 1024, A.add)
+    ts(PAR4, PAR, 4.0, A.mult, "pf", "par4")
+    ts(R16, R_, 16.0, A.mult, "pf", "r16", 15.0, A.add)
+    ts(T.mask2[:], T.y16[:], R_, A.not_equal, "y16 pf", "mask2", BIG, A.mult)
+    ts(T.m0[:], T.y16[:], R_, A.is_equal, "y16 pf s1024", "m0", S1024, A.mult)
+    ts(T.endu[:], T.y16[:, 0:4], 0.0, A.mult, "y16 r16", "endu", R16, A.add)
+    ts(T.nb[:, 0:5], T.jf[:, 1:6], R4, A.add, "jf r4", "nb", -256.0, A.mult)
+    ts(T.node2[:, 0:16], T.jf[:, 0:256:16], R_, A.add, "jf pf", "node2a")
+    ts(T.node2[:, 16:32], T.jf[:, 0:256:16], R_, A.add, "jf pf", "node2b")
+    cp(T.ulu[:, 0:8], T.jf[:, 0:128:16], "jf", "ulua")
+    cp(T.ulu[:, 8:16], T.jf[:, 1:128:16], "jf", "ulub")
+
+    qz(T.sq0[:], T.ss0[:], T.xb[:], "xb", "s0")
+    send(u8(T.lq0[:]), u8(T.sq0[:]), "arr0", "s0")
+    send(T.ls0[:], T.ss0[:], "arr0", "s0")
+    wait("y", ("sent", total["sent"]))
+    dma("y", "dw", 32, u8(T.wq[:]), T.wc[:], "", "w")
+    dma("y", "dw", 32, T.wsc[:], T.ws[:], "", "w")
+    dma("y", "dv", 16, T.vb[:], T.v[:], "", "vb")
+    op("g", lambda: g.affine_select(T.c1[:], T.ones[:], [[1, 514]], A.is_equal, 0.0, -3, -4), "ones", "c1")
+    iota(T.tb[:, 0:4], [[1, 4]], 0, 0, "tba")
+    iota(T.tb[:, 4:8], [[-1, 4]], 0, 0, "tbb")
+    iota(T.g8[:], [[1, 8], [0, 64]], 0, 0, "g8")
+    iota(T.mt[:, 4096:5120], [[0, 1024]], 0, 0, "m16")
+
+    def own_gather(t):
+        w = (3 - t) * 1024
+        act(T.own[:], T.ring[:, w:w + 4096].indirect(T.ownu[:]), ACT.Copy,
+            "ringx ownu " + four("rx%d") + "".join(" " + four("h" + str(k) + "_%d") for k in range(t)), "own", scale=0.5)
+
+    ts(T.t1[:], T.if_[:], 1024.0, A.mult, "if", "t1")
+    ts(T.t2[:], T.ia[:], 4.0, A.mult, "ia", "t2")
+    ts(T.t64[:], T.im[:], 64.0, A.mult, "im", "t64")
+    tt(T.t3[:], T.t1[:], T.t2[:], A.add, "t1 t2", "t3")
+    tt(T.o0[:], T.t64[:], T.ib[:], A.add, "t64 ib", "o0")
+    cp(T.au[:], T.ia[:], "ia", "au")
+    for b in range(4):
+        ts(T.off0[:, 16 * b:16 * b + 16], T.t3[:], float(b), A.add, "t3", "off0_%d" % b)
+    cp(T.faru[:, 0:16], T.o0[:], "o0", "faru0")
+    cp(T.ownu[:], T.off0[:], four("off0_%d"), "ownu off0")
+    ts(T.fu[:], T.if_[:], PAR4, A.add, "if par4", "fu")
+    qz(T.uq[:], T.us[:], T.ub[:], "ub", "uq")
+    qz(*pair("eq", "es", 0, 128), T.c0[:, 2:514], "c0", "E0")
+    qz(*pair("eq", "es", 256, 384), T.c0[:, 0:512], "c0", "E2")
+    cp(T.wv[:].indirect(T.au[:]), T.jf[:], "au jf", "wv")
+    cp(T.uq2[:].bitcast(dt.uint32), T.uq[:].bitcast(dt.uint32).indirect(T.ulu[:]), "uq ulua ulub", "uq2")
+    act(T.us2[:], T.us[:].indirect(T.ulu[:]), ACT.Copy, "uq ulua ulub", "us2")
+    own_gather(0)
+    tt(T.ym[:], T.wv[:], T.m0[:], A.mult, "wv m0", "ym")
+    qz(*pair("eq", "es", 128, 256), T.c1[:, 2:514], "c1", "E1")
+    qz(*pair("eq", "es", 384, 512), T.c1[:, 0:512], "c1", "E3")
+    scan(T.ys[:], T.keep[:], T.ym[:], A.mult, A.add, "keep ym", "ys")
+    cp(T.ac[:, 0:16], T.ia[:], "ia", "aca")
+    ts(T.bi[:, 0:16], T.ib[:], 3, A.bitwise_and, "ib", "bia")
+    ts(T.ac[:, 16:32], T.ys[:, 15:256:16], SINV, A.mult, "ys sinv", "acb")
+    ts(T.bi[:, 16:32], T.ib[:], 2, A.logical_shift_right, "ib", "bib")
+    act(T.fr[:], T.tb[:, 0:8].indirect(T.fu[:]), ACT.Copy, "tba tbb fu", "fr")
+    cp(T.cu[:], T.ac[:, 16:32], "acb", "cu")
+    tt(T.xx[:], T.ac[:], T.node2[:], A.subtract, "aca acb node2a node2b", "xx")
+    ts(T.t5[:], T.bi[:, 0:16], 5.0, A.mult, "bia", "t5")
+    act(T.er0[:], T.fr[:].indirect(T.cu[:]), ACT.Copy, "fr cu", "er0")
+    ts(T.t0[:], T.xx[:], PAR, A.mult, "xx pf", "t0")
+    tt(T.dp[:], T.t5[:], T.bi[:, 16:32], A.subtract, "t5 bib", "dp")
+    ts(T.mk[:, 0:16], T.im[:], 1.0, A.is_lt, "im", "mka", 3.0, A.mult)
+    ts(T.mk[:, 16:32], T.im[:], 2.0, A.is_lt, "im", "mkb", 3.0, A.mult)
+    tt(T.ll[:, 0:32], T.t0[:], T.node2[:], A.add, "t0 node2a node2b", "lla")
+    tt(T.ll[:, 32:64], T.ac[:], T.t0[:], A.subtract, "t0 aca acb", "llb")
+    tt(T.mk2[:, 0:16], T.mk[:, 0:16], T.dp[:], A.mult, "mka dp", "mk2a")
+    tt(T.mk2[:, 16:32], T.mk[:, 16:32], T.dp[:], A.mult, "mkb dp", "mk2b")
+    cp(T.llu[:], T.ll[:], "lla llb", "llu")
+    ts(T.e0[:, 0:256:2], T.fr[:, 0:256:2], -3.0, A.add, "fr", "e0a")
+    ts(T.e0[:, 1:256:2], T.fr[:, 1:256:2], 3.0, A.add, "fr", "e0b")
+    tt(T.mk3[:, 0:16], T.mk2[:, 0:16], T.o0[:], A.add, "mk2a o0", "mk3a")
+    tt(T.mk3[:, 16:32], T.mk2[:, 16:32], T.o0[:], A.add, "mk2b o0", "mk3b")
+    ts(T.gt[:], T.g8[:], G_, A.is_equal, "g8 pf", "gt", 256.0, A.mult)
+    tt(T.mx[:], T.e0[:, 0:256:2], T.er0[:, 0:256:2], A.max, "e0a er0", "mx")
+    tt(T.mn[:], T.e0[:, 0:256:2], T.er0[:, 0:256:2], A.min, "e0a er0", "mn")
+    cp(T.faru[:, 16:48], T.mk3[:], "mk3a mk3b", "faru1 faru2")
+    qz(T.gq[:], T.gs[:], T.gt[:], "gt", "gq")
+    ts(T.hi[:], T.mx[:], -1.0, A.mult, "mx", "hi")
+    ts(T.lo[:], T.mn[:], -1.0, A.mult, "mn", "lo", -3.0, A.add)
+
+    def unpack(t):
+        for b in range(4):
+            mm(2 + b, pair("eq", "es", 128 * b, 128 * b + 128), pair("lq%d" % t, "ls%d" % t, 0, C), "E%d l%d" % (b, t))
+
+    unpack(0)
+    for b in range(4):
+        scaled("v" if b == 0 else "s", T.bord[:, 384 * b + 128:384 * b + 384], 2 + b, 0.5, "bx%d" % b)
+
+    slots = DIRECT + SIGNED
+    UO, UL, ZT = pair("uq2", "us2", 0, 128), pair("uq2", "us2", 128, 256), pair("zq", "zs", 0, C)
+
+    def wb(b):
+        return pair("wq", "wsc", 128 * b, 128 * b + 128)
+
+    def row(c, a, b):
+        s = slots.index(c)
+        base = 1024 * (s // 4) + s % 4
+        return T.mt[:, base + 4 * a:base + 4 * (b - 1) + 1:4]
+
+    def sum_tile(k, first, last):
+        names = "m16" if k == 4 else " ".join("m%d%s" % (slots[4 * k + i], h) for i in range(4) for h in "ab")
+        m = pair("mq", "ms", 256 * k, 256 * k + 256)
+        qz(*m, T.mt[:, 1024 * k:1024 * k + 1024], names, "mq%d" % k)
+        mm(6, pair("gq", "gs", 0, 128), m, "gq mq%d" % k, first, last)
+
+    def picked(t):
+        for b in range(4):
+            o = T.bord[:, 384 * b + 64 * (2 - t):384 * b + 64 * (3 - t)]
+            w = T.dpl[:, 256 * b:256 * b + 256].indirect(T["el%d" % t][:])
+            rd, wr = "dpl%d el%d" % (b, t), "b%d_%d" % (t, b)
+            if b == 0:
+                cp(o, w, rd, wr)
+            else:
+                act(o, w, ACT.Copy, rd, wr)
+
+    def reading(t, a, e, name):
+        for b in range(4):
+            w0 = 384 * b + 64 * (2 - t)
+            tt(T.z[:, 4 * a + b:4 * e:4], T.bord[:, w0:w0 + 256].indirect(T.faru[:, 16 * t + a // 16:16 * t + e // 16]),
+               T.own[:, 256 * b + a:256 * b + e], A.add,
+               "bx%d own faru%d " % (b, t) + " ".join("b%d_%d" % (k, b) for k in range(1, t + 1)), "z%d%s" % (b, name[0]))
+        qz(*pair("zq", "zs", a, e), T.z[:, 4 * a:4 * e], four("z%d" + name[0]), " ".join("zq" + h for h in name))
+
+    for t in range(2):
+        if t > 0:
+            picked(t)
+        reading(t, 0, C, "AB")
+        mm(0, UO, ZT, "uq2 us2 zqA")
+        for b in range(4):
+            mm(2 + b, wb(b), ZT, "w zqA")
+        mm(7, UO, ZT, "uq2 us2 zqA")
+        mm(1, UL, ZT, "uq2 us2 zqA zqB")
+        h0 = (2 - t) * 1024
+        sq, ss, u = T["sq%d" % (t + 1)], T["ss%d" % (t + 1)], t + 1
+        for b in range(4):
+            scaled("s", T.ring[:, h0 + b:h0 + 1024:4], 2 + b, 0.03125, "h%d_%d" % (t, b))
+        act(T.sg[:], T.ps[:, 512 + t:512 + C:2], ACT.Sign, "ps1", "sg")
+
+        tt(T.d1[:], bank(0), T.mask2[:], A.add, "ps0 mask2", "d1")
+        scan(T.sc[:], T.reset[:], T.d1[:], A.add, A.min, "reset d1", "sc")
+        tt(T.mt[:, 4096:5120:4], bank(0), T.sc[:], A.is_equal, "ps0 sc", "m16")
+        for c in SIGNED:
+            act(row(c, 0, C), bank(7), ACT.Sign, "ps7 sc", "m%da m%db" % (c, c), bias=T.sc[:, 16 * c + 15:16 * c + 16], scale=-1.0)
+        for i, c in enumerate(DIRECT):
+            e = 16 * c + 16
+            col = T.sc[:, e - 1:e]
+            ts(row(c, 0, e), T.ps[:, 0:e], col, A.is_lt, "ps0 sc", "m%da" % c)
+            if e < C:
+                ts(row(c, e, C), T.ps[:, e:C], col, A.is_le, "ps0 sc", "m%db" % c)
+            if i == 0:
+                sum_tile(4, True, False)
+            if i == 2:
+                qz(sq[:], ss[:], T.ring[:, h0:h0 + 1024], four("h" + str(t) + "_%d"), "s%d" % u)
+                send(u8(T["lq%d" % u][:]), u8(sq[:]), "arr%d" % u, "s%d" % u)
+                send(T["ls%d" % u][:], ss[:], "arr%d" % u, "s%d" % u)
+        for k in range(len(DIRECT) // 4):
+            sum_tile(k, False, False)
+        pend = []
+        for c in SIGNED:
+            e = 16 * c + 16
+            ts(row(c, 0, e), row(c, 0, e), 0.0, A.is_gt, "m%da" % c, "m%da" % c)
+            if e < C:
+                ts(row(c, e, C), row(c, e, C), 0.0, A.is_ge, "m%db" % c, "m%db" % c)
+            for k in pend:
+                sum_tile(k, False, False)
+            s = slots.index(c)
+            pend = [s // 4] if s % 4 == 3 else []
+        sum_tile(3, False, True)
+        tt(T.tm[:], T.sg[:], T.hi[:], A.min, "sg hi", "tm")
+        tt(T.key[:], bank(6), T.jf[:], A.add, "ps6 jf", "key")
+        for c in range(3):
+            act(T.junk[:, 256 * c:256 * c + 256], T.key[:], ACT.Relu, "key nb", "junk%d ff%d" % (c, c),
+                bias=T.nb[:, c:c + 1], accum_out=T.ff[:, c:c + 1])
+        for c in (3, 4):
+            ts(T.junkv[:, 256 * (c - 3):256 * (c - 2)], T.key[:], T.nb[:, c:c + 1], A.add, "key nb", "junk%d" % c, 0.0, A.max)
+        for c in (3, 4):
+            op("v", lambda: V.tensor_reduce(T.ff[:, c:c + 1], T.junkv[:, 256 * (c - 3):256 * (c - 2)], AxisListType.X, A.add),
+               "junk%d" % c, "ff%d" % c)
+        tt(T.fd[:], T.ff[:, 0:4], T.ff[:, 1:5], A.subtract, "ff4 " + four("ff%d"), "fd")
+        tt(T.fe[:], T.fd[:], T.nb[:, 0:4], A.subtract, "fd nb", "fe")
+        ts(T["eo%d" % u][:], T.fe[:], -65536.0, A.add, "fe", "eo%d" % u)
+        send(T["el%d" % u][:], T["eo%d" % u][:], "lst%d" % u, "eo%d" % u)
+
+        unpack(u)
+        for b in range(4):
+            scaled("s", T.dpl[:, 256 * b:256 * b + 256], 2 + b, 0.5, "dpl%d" % b)
+        tt(T.lf[:, t:256:2], T.tm[:], T.lo[:], A.max, "tm lo", "lf")
+        la_, lc_ = T.llu[:, 32 * t:32 * t + 16], T.llu[:, 32 * t + 16:32 * t + 32]
+        tt(T.ym[:], T.lf[:].indirect(la_), T.m0[:], A.mult, "lf llu m0", "ym")
+        scan(T.ys[:], T.keep[:], T.ym[:], A.mult, A.add if t == 0 else A.subtract, "keep ym", "ys")
+        tt(T["off%d" % u][:], T.ys[:].indirect(T.endu[:]), T["off%d" % t][:], A.add, "ys endu off%d" % t, "off%d" % u)
+        cp(T.ownu[:], T["off%d" % u][:], "off%d" % u, "ownu")
+        own_gather(u)
+        o = A.add if t == 0 else A.subtract
+        tt(T["e%d" % u][:], T.lf[:].indirect(la_), T["e%d" % t][:], o, "lf llu e0a e0b e1", "e%d" % u)
+        tt(T["er%d" % u][:], T.lf[:].indirect(lc_), T["er%d" % t][:], o, "lf llu er%d" % t, "er%d" % u)
+        a_, b_, nm = T["e%d" % u][:, 1 - t:256:2], T["er%d" % u][:, 1 - t:256:2], "e%d er%d" % (u, u)
+        tt(T.mx[:], a_, b_, A.max, nm, "mx")
+        tt(T.hi[:], a_, b_, A.min, nm, "hi")
+        ts(T.lo[:], T.mx[:], -3.0, A.add, "mx", "lo")
+        if t == 1:
+            qz(T.vq[:], T.vs[:], T.vb[:], "vb", "vq")
+
+    picked(2)
+    VQ = pair("vq", "vs", 0, 128)
+    reading(2, 0, 128, "A")
+    for b in range(4):
+        mm(2 + b, wb(b), pair("zq", "zs", 0, 128), "w zqA", w=128)
+        scaled("s", T.ring[:, b:512:4], 2 + b, 0.03125, "hA%d" % b, 128)
+    reading(2, 128, C, "B")
+    second = (0, 6, 7, 2)
+    for b in range(4):
+        mm(second[b], wb(b), pair("zq", "zs", 128, C), "w zqB", w=128)
+    mm(1, UL, ZT, "uq2 us2 zqA zqB")
+    qz(*pair("sq3", "ss3", 0, 128), T.ring[:, 0:512], four("hA%d"), "sA")
+    mm(3, VQ, pair("sq3", "ss3", 0, 128), "vq sA", w=128)
+    dma("y", "dout", 144, T.oc[:, 0:512], u8(T.sq3[:, 0:128]), "sA", "")
+    for b in range(4):
+        scaled("vs"[b % 2], T.ring[:, 512 + b:1024:4], second[b], 0.03125, "hB%d" % b, 128)
+    act(T.sg[:], T.ps[:, 512:512 + C:2], ACT.Sign, "ps1", "sg")
+    qz(*pair("sq3", "ss3", 128, C), T.ring[:, 512:1024], four("hB%d"), "sB")
+    mm(4, VQ, pair("sq3", "ss3", 128, C), "vq sB", w=128)
+    act(T.yo[:, 0:128], bank(3, 128), ACT.Copy, "ps3", "yA")
+    dma("y", "dout", 144, T.oc[:, 512:1024], u8(T.sq3[:, 128:256]), "sB", "")
+    dma("y", "dout", 144, T.y[:, 0:128], T.yo[:, 0:128], "yA", "")
+    for k in range(4):
+        dma("y" if k < 2 else "s", "dout", 144, T.osc[4 * k:4 * k + 4, :], T.ss3[32 * k:32 * k + 4, :], "sA sB", "")
+    tt(T.tm[:], T.sg[:], T.hi[:], A.min, "sg hi", "tm")
+    act(T.yo[:, 128:256], bank(4, 128), ACT.Copy, "ps4", "yB")
+    dma("s", "dout", 144, T.y[:, 128:256], T.yo[:, 128:256], "yB", "")
+    tt(T.d2[:], T.tm[:], T.lo[:], A.max, "tm lo", "d2")
+    tt(T.lf[:, 0:256:2], T.lf[:, 0:256:2], T.d2[:], A.add, "d2 lf", "lf")
+    dma("y", "dout", 144, T.ol[:], T.lf[0:128:16, :], "lf", "")
+
+    for s in total:
+        if waited.get(s, 0) < total[s]:
+            wait("g", (s, total[s]))

@@ -16,7 +16,7 @@ for _d, _names in (
              "wv:256 fr:256 e0:256 er0:256 e1:256 er1:256 e2:256 er2:256 hi:128 lo:128 mx:128 mn:128 sg:128 tm:128 d2:128 ym:256 ys:256 "
              "own:1024 z:1024 dpl:1024 bord:1536 mt:5120"),
         (F32, "pf:8 jf:256 nb:8 node2:32 t1:16 t2:16 t3:16 off0:64 off1:64 off2:64 o0:16 dp:16 t5:16 mk:32 mk2:32 mk3:32 t64:16 ac:32 xx:32 "
-              "t0:32 ll:64 lf:256 d1:256 sc:256 key:256 junk:768 junkv:512 ff:8 fd:4 fe:4 yo:256")):
+              "t0:32 ll:64 lf:256 d1:256 sc:256 key:260 junk:1040 junkv:260 ff:8 fd:4 yo:256")):
     for _e in _names.split():
         SCRATCH[_e.split(":")[0]] = ("sbuf", [128, int(_e.split(":")[1])], _d)
 SEMAPHORES = ["cv", "cs", "ct", "cg", "sent", "arr0", "arr1", "arr2", "lst1", "lst2",
@@ -157,11 +157,11 @@ def rank_program(g, core, T, topo):
 
     for k in range(4):
         dma("y" if k < 2 else "s", "dxb", 64, T.xb[:, 256 * k:256 * k + 256], T.x[:, 1024 * k:1024 * k + 256], "", "xb")
-    dma("s", "dla", 16, T.ia[:], T.la[:], "", "ia")
+    dma("y", "dla", 16, T.ia[:], T.la[:], "", "ia")
     dma("s", "dda", 16, T.if_[:], T.da[:], "", "if")
-    dma("s", "dlb", 16, T.ib[:], T.lb[:], "", "ib")
+    dma("y", "dlb", 16, T.ib[:], T.lb[:], "", "ib")
     dma("s", "ddb", 16, T.im[:], T.db[:], "", "im")
-    dma("y", "du", 16, T.ub[:], T.u[:], "", "ub")
+    dma("s", "du", 16, T.ub[:], T.u[:], "", "ub")
     for k in range(4):
         dma("y", "dx", 64, T.ring[:, 3072 + 1024 * k + 256:4096 + 1024 * k], T.x[:, 1024 * k + 256:1024 * k + 1024], "", "ringx")
     for k in range(4):
@@ -189,6 +189,7 @@ def rank_program(g, core, T, topo):
     ts(T.m0[:], T.y16[:], R_, A.is_equal, "y16 pf s1024", "m0", S1024, A.mult)
     ts(T.endu[:], T.y16[:, 0:4], 0.0, A.mult, "y16 r16", "endu", R16, A.add)
     ts(T.nb[:, 0:5], T.jf[:, 1:6], R4, A.add, "jf r4", "nb", -256.0, A.mult)
+    ts(T.key[:, 256:260], T.jf[:, 0:4], 257.0, A.add, "jf", "keyx", 256.0, A.mult)
     ts(T.node2[:, 0:16], T.jf[:, 0:256:16], R_, A.add, "jf pf", "node2a")
     ts(T.node2[:, 16:32], T.jf[:, 0:256:16], R_, A.add, "jf pf", "node2b")
     cp(T.ulu[:, 0:8], T.jf[:, 0:128:16], "jf", "ulua")
@@ -212,36 +213,36 @@ def rank_program(g, core, T, topo):
         act(T.own[:], T.ring[:, w:w + 4096].indirect(T.ownu[:]), ACT.Copy,
             "ringx ownu " + four("rx%d") + "".join(" " + four("h" + str(k) + "_%d") for k in range(t)), "own", scale=0.5)
 
-    ts(T.t1[:], T.if_[:], 1024.0, A.mult, "if", "t1")
-    ts(T.t2[:], T.ia[:], 4.0, A.mult, "ia", "t2")
-    ts(T.t64[:], T.im[:], 64.0, A.mult, "im", "t64")
-    tt(T.t3[:], T.t1[:], T.t2[:], A.add, "t1 t2", "t3")
-    tt(T.o0[:], T.t64[:], T.ib[:], A.add, "t64 ib", "o0")
     cp(T.au[:], T.ia[:], "ia", "au")
-    for b in range(4):
-        ts(T.off0[:, 16 * b:16 * b + 16], T.t3[:], float(b), A.add, "t3", "off0_%d" % b)
-    cp(T.faru[:, 0:16], T.o0[:], "o0", "faru0")
-    cp(T.ownu[:], T.off0[:], four("off0_%d"), "ownu off0")
-    ts(T.fu[:], T.if_[:], PAR4, A.add, "if par4", "fu")
-    qz(T.uq[:], T.us[:], T.ub[:], "ub", "uq")
     qz(*pair("eq", "es", 0, 128), T.c0[:, 2:514], "c0", "E0")
     qz(*pair("eq", "es", 256, 384), T.c0[:, 0:512], "c0", "E2")
+    ts(T.t2[:], T.ia[:], 4.0, A.mult, "ia", "t2")
+    ts(T.t1[:], T.if_[:], 1024.0, A.mult, "if", "t1")
     cp(T.wv[:].indirect(T.au[:]), T.jf[:], "au jf", "wv")
-    cp(T.uq2[:].bitcast(dt.uint32), T.uq[:].bitcast(dt.uint32).indirect(T.ulu[:]), "uq ulua ulub", "uq2")
+    tt(T.t3[:], T.t1[:], T.t2[:], A.add, "t1 t2", "t3")
+    ts(T.fu[:], T.if_[:], PAR4, A.add, "if par4", "fu")
+    for b in range(4):
+        ts(T.off0[:, 16 * b:16 * b + 16], T.t3[:], float(b), A.add, "t3", "off0_%d" % b)
+    qz(T.uq[:], T.us[:], T.ub[:], "ub", "uq")
+    cp(T.ownu[:], T.off0[:], four("off0_%d"), "ownu off0")
+    tt(T.ym[:], T.wv[:], T.m0[:], A.mult, "wv m0", "ym")
     act(T.us2[:], T.us[:].indirect(T.ulu[:]), ACT.Copy, "uq ulua ulub", "us2")
     own_gather(0)
-    tt(T.ym[:], T.wv[:], T.m0[:], A.mult, "wv m0", "ym")
-    qz(*pair("eq", "es", 128, 256), T.c1[:, 2:514], "c1", "E1")
-    qz(*pair("eq", "es", 384, 512), T.c1[:, 0:512], "c1", "E3")
+    ts(T.t64[:], T.im[:], 64.0, A.mult, "im", "t64")
     scan(T.ys[:], T.keep[:], T.ym[:], A.mult, A.add, "keep ym", "ys")
+    tt(T.o0[:], T.t64[:], T.ib[:], A.add, "t64 ib", "o0")
     cp(T.ac[:, 0:16], T.ia[:], "ia", "aca")
-    ts(T.bi[:, 0:16], T.ib[:], 3, A.bitwise_and, "ib", "bia")
     ts(T.ac[:, 16:32], T.ys[:, 15:256:16], SINV, A.mult, "ys sinv", "acb")
-    ts(T.bi[:, 16:32], T.ib[:], 2, A.logical_shift_right, "ib", "bib")
-    act(T.fr[:], T.tb[:, 0:8].indirect(T.fu[:]), ACT.Copy, "tba tbb fu", "fr")
+    cp(T.faru[:, 0:16], T.o0[:], "o0", "faru0")
+    ts(T.bi[:, 0:16], T.ib[:], 3, A.bitwise_and, "ib", "bia")
     cp(T.cu[:], T.ac[:, 16:32], "acb", "cu")
+    ts(T.bi[:, 16:32], T.ib[:], 2, A.logical_shift_right, "ib", "bib")
     tt(T.xx[:], T.ac[:], T.node2[:], A.subtract, "aca acb node2a node2b", "xx")
     ts(T.t5[:], T.bi[:, 0:16], 5.0, A.mult, "bia", "t5")
+    cp(T.uq2[:].bitcast(dt.uint32), T.uq[:].bitcast(dt.uint32).indirect(T.ulu[:]), "uq ulua ulub", "uq2")
+    qz(*pair("eq", "es", 128, 256), T.c1[:, 2:514], "c1", "E1")
+    qz(*pair("eq", "es", 384, 512), T.c1[:, 0:512], "c1", "E3")
+    act(T.fr[:], T.tb[:, 0:8].indirect(T.fu[:]), ACT.Copy, "tba tbb fu", "fr")
     act(T.er0[:], T.fr[:].indirect(T.cu[:]), ACT.Copy, "fr cu", "er0")
     ts(T.t0[:], T.xx[:], PAR, A.mult, "xx pf", "t0")
     tt(T.dp[:], T.t5[:], T.bi[:, 16:32], A.subtract, "t5 bib", "dp")
@@ -252,17 +253,11 @@ def rank_program(g, core, T, topo):
     tt(T.mk2[:, 0:16], T.mk[:, 0:16], T.dp[:], A.mult, "mka dp", "mk2a")
     tt(T.mk2[:, 16:32], T.mk[:, 16:32], T.dp[:], A.mult, "mkb dp", "mk2b")
     cp(T.llu[:], T.ll[:], "lla llb", "llu")
-    ts(T.e0[:, 0:256:2], T.fr[:, 0:256:2], -3.0, A.add, "fr", "e0a")
-    ts(T.e0[:, 1:256:2], T.fr[:, 1:256:2], 3.0, A.add, "fr", "e0b")
     tt(T.mk3[:, 0:16], T.mk2[:, 0:16], T.o0[:], A.add, "mk2a o0", "mk3a")
     tt(T.mk3[:, 16:32], T.mk2[:, 16:32], T.o0[:], A.add, "mk2b o0", "mk3b")
     ts(T.gt[:], T.g8[:], G_, A.is_equal, "g8 pf", "gt", 256.0, A.mult)
-    tt(T.mx[:], T.e0[:, 0:256:2], T.er0[:, 0:256:2], A.max, "e0a er0", "mx")
-    tt(T.mn[:], T.e0[:, 0:256:2], T.er0[:, 0:256:2], A.min, "e0a er0", "mn")
     cp(T.faru[:, 16:48], T.mk3[:], "mk3a mk3b", "faru1 faru2")
     qz(T.gq[:], T.gs[:], T.gt[:], "gt", "gq")
-    ts(T.hi[:], T.mx[:], -1.0, A.mult, "mx", "hi")
-    ts(T.lo[:], T.mn[:], -1.0, A.mult, "mn", "lo", -3.0, A.add)
 
     def unpack(t):
         for b in range(4):
@@ -318,12 +313,21 @@ def rank_program(g, core, T, topo):
         mm(1, UL, ZT, "uq2 us2 zqA zqB")
         h0 = (2 - t) * 1024
         sq, ss, u = T["sq%d" % (t + 1)], T["ss%d" % (t + 1)], t + 1
+        if t == 0:
+            act(T.e0[:, 0:256:2], T.fr[:, 0:256:2], ACT.Identity, "fr", "e0a", bias=-3.0)
+            act(T.e0[:, 1:256:2], T.fr[:, 1:256:2], ACT.Identity, "fr", "e0b", bias=3.0)
         for b in range(4):
             scaled("s", T.ring[:, h0 + b:h0 + 1024:4], 2 + b, 0.03125, "h%d_%d" % (t, b))
-        act(T.sg[:], T.ps[:, 512 + t:512 + C:2], ACT.Sign, "ps1", "sg")
+        act(T.sg[:], T.ps[:, 512 + t:512 + C:2], ACT.Sign, "ps1", "sg", scale=-1.0 if t == 0 else 1.0)
 
+        if t == 0:
+            tt(T.hi[:], T.e0[:, 0:256:2], T.er0[:, 0:256:2], A.max, "e0a er0", "hi")
         tt(T.d1[:], bank(0), T.mask2[:], A.add, "ps0 mask2", "d1")
+        if t == 0:
+            tt(T.mn[:], T.e0[:, 0:256:2], T.er0[:, 0:256:2], A.min, "e0a er0", "mn")
         scan(T.sc[:], T.reset[:], T.d1[:], A.add, A.min, "reset d1", "sc")
+        if t == 0:
+            ts(T.lo[:], T.mn[:], 3.0, A.add, "mn", "lo")
         tt(T.mt[:, 4096:5120:4], bank(0), T.sc[:], A.is_equal, "ps0 sc", "m16")
         for c in SIGNED:
             act(row(c, 0, C), bank(7), ACT.Sign, "ps7 sc", "m%da m%db" % (c, c), bias=T.sc[:, 16 * c + 15:16 * c + 16], scale=-1.0)
@@ -352,58 +356,65 @@ def rank_program(g, core, T, topo):
             s = slots.index(c)
             pend = [s // 4] if s % 4 == 3 else []
         sum_tile(3, False, True)
-        tt(T.tm[:], T.sg[:], T.hi[:], A.min, "sg hi", "tm")
-        tt(T.key[:], bank(6), T.jf[:], A.add, "ps6 jf", "key")
-        for c in range(3):
-            act(T.junk[:, 256 * c:256 * c + 256], T.key[:], ACT.Relu, "key nb", "junk%d ff%d" % (c, c),
+        tt(T.tm[:], T.sg[:], T.hi[:], A.max if t == 0 else A.min, "sg hi", "tm")
+        tt(T.key[:, 0:C], bank(6), T.jf[:], A.add, "ps6 jf", "key")
+        for c in range(4):
+            act(T.junk[:, 260 * c:260 * c + C + c], T.key[:, 0:C + c], ACT.Relu, "key keyx nb", "junk%d ff%d" % (c, c),
                 bias=T.nb[:, c:c + 1], accum_out=T.ff[:, c:c + 1])
-        for c in (3, 4):
-            ts(T.junkv[:, 256 * (c - 3):256 * (c - 2)], T.key[:], T.nb[:, c:c + 1], A.add, "key nb", "junk%d" % c, 0.0, A.max)
-        for c in (3, 4):
-            op("v", lambda: V.tensor_reduce(T.ff[:, c:c + 1], T.junkv[:, 256 * (c - 3):256 * (c - 2)], AxisListType.X, A.add),
-               "junk%d" % c, "ff%d" % c)
+        la_, lc_ = T.llu[:, 32 * t:32 * t + 16], T.llu[:, 32 * t + 16:32 * t + 32]
+        tt(T.lf[:, t:256:2], T.tm[:], T.lo[:], A.min if t == 0 else A.max, "tm lo", "lf")
+        ts(T.junkv[:], T.key[:], T.nb[:, 4:5], A.add, "key keyx nb", "junk4", 0.0, A.max)
+        tt(T.ym[:], T.lf[:].indirect(la_), T.m0[:], A.mult, "lf llu m0", "ym")
+        op("v", lambda: V.tensor_reduce(T.ff[:, 4:5], T.junkv[:], AxisListType.X, A.add), "junk4", "ff4")
+        scan(T.ys[:], T.keep[:], T.ym[:], A.mult, A.subtract, "keep ym", "ys")
         tt(T.fd[:], T.ff[:, 0:4], T.ff[:, 1:5], A.subtract, "ff4 " + four("ff%d"), "fd")
-        tt(T.fe[:], T.fd[:], T.nb[:, 0:4], A.subtract, "fd nb", "fe")
-        ts(T["eo%d" % u][:], T.fe[:], -65536.0, A.add, "fe", "eo%d" % u)
+        tt(T["off%d" % u][:], T.ys[:].indirect(T.endu[:]), T["off%d" % t][:], A.add, "ys endu off%d" % t, "off%d" % u)
+        cp(T["eo%d" % u][:], T.fd[:], "fd", "eo%d" % u)
         send(T["el%d" % u][:], T["eo%d" % u][:], "lst%d" % u, "eo%d" % u)
 
         unpack(u)
-        for b in range(4):
-            scaled("s", T.dpl[:, 256 * b:256 * b + 256], 2 + b, 0.5, "dpl%d" % b)
-        tt(T.lf[:, t:256:2], T.tm[:], T.lo[:], A.max, "tm lo", "lf")
-        la_, lc_ = T.llu[:, 32 * t:32 * t + 16], T.llu[:, 32 * t + 16:32 * t + 32]
-        tt(T.ym[:], T.lf[:].indirect(la_), T.m0[:], A.mult, "lf llu m0", "ym")
-        scan(T.ys[:], T.keep[:], T.ym[:], A.mult, A.add if t == 0 else A.subtract, "keep ym", "ys")
-        tt(T["off%d" % u][:], T.ys[:].indirect(T.endu[:]), T["off%d" % t][:], A.add, "ys endu off%d" % t, "off%d" % u)
         cp(T.ownu[:], T["off%d" % u][:], "off%d" % u, "ownu")
         own_gather(u)
-        o = A.add if t == 0 else A.subtract
-        tt(T["e%d" % u][:], T.lf[:].indirect(la_), T["e%d" % t][:], o, "lf llu e0a e0b e1", "e%d" % u)
-        tt(T["er%d" % u][:], T.lf[:].indirect(lc_), T["er%d" % t][:], o, "lf llu er%d" % t, "er%d" % u)
-        a_, b_, nm = T["e%d" % u][:, 1 - t:256:2], T["er%d" % u][:, 1 - t:256:2], "e%d er%d" % (u, u)
-        tt(T.mx[:], a_, b_, A.max, nm, "mx")
-        tt(T.hi[:], a_, b_, A.min, nm, "hi")
-        ts(T.lo[:], T.mx[:], -3.0, A.add, "mx", "lo")
-        if t == 1:
+        for b in range(4):
+            scaled("v" if b < 2 else "s", T.dpl[:, 256 * b:256 * b + 256], 2 + b, 0.5, "dpl%d" % b)
+        if t == 0:
+            tt(T.e1[:], T.lf[:].indirect(la_), T.e0[:], A.subtract, "lf llu e0a e0b", "e1")
+            tt(T.er1[:], T.lf[:].indirect(lc_), T.er0[:], A.subtract, "lf llu er0", "er1")
+            a_, b_ = T.e1[:, 1:256:2], T.er1[:, 1:256:2]
+            tt(T.mx[:], a_, b_, A.max, "e1 er1", "mx")
+            tt(T.mn[:], a_, b_, A.min, "e1 er1", "mn")
+            ts(T.hi[:], T.mx[:], -1.0, A.mult, "mx", "hi")
+            ts(T.lo[:], T.mn[:], -1.0, A.mult, "mn", "lo", -3.0, A.add)
+        else:
+            tt(T.e2[:], T.lf[:].indirect(la_), T.e1[:], A.add, "lf llu e1", "e2")
+            tt(T.er2[:], T.lf[:].indirect(lc_), T.er1[:], A.add, "lf llu er1", "er2")
+            a_, b_ = T.e2[:, 0:256:2], T.er2[:, 0:256:2]
+            tt(T.mx[:], a_, b_, A.max, "e2 er2", "mx")
+            tt(T.hi[:], a_, b_, A.min, "e2 er2", "hi")
+            ts(T.lo[:], T.mx[:], -3.0, A.add, "mx", "lo")
             qz(T.vq[:], T.vs[:], T.vb[:], "vb", "vq")
 
     picked(2)
     VQ = pair("vq", "vs", 0, 128)
+    ZA, ZB = pair("zq", "zs", 0, 128), pair("zq", "zs", 128, C)
     reading(2, 0, 128, "A")
     for b in range(4):
-        mm(2 + b, wb(b), pair("zq", "zs", 0, 128), "w zqA", w=128)
+        mm(2 + b, wb(b), ZA, "w zqA", w=128)
         scaled("s", T.ring[:, b:512:4], 2 + b, 0.03125, "hA%d" % b, 128)
+    mm(1, UL, ZA, "uq2 us2 zqA", w=128)
+    act(T.sg[:, 0:64], T.ps[:, 512:512 + 128:2], ACT.Sign, "ps1", "sg")
     reading(2, 128, C, "B")
     second = (0, 6, 7, 2)
+    mm(5, UL, ZB, "uq2 us2 zqB", w=128)
     for b in range(4):
-        mm(second[b], wb(b), pair("zq", "zs", 128, C), "w zqB", w=128)
-    mm(1, UL, ZT, "uq2 us2 zqA zqB")
+        mm(second[b], wb(b), ZB, "w zqB", w=128)
+    act(T.sg[:, 64:128], T.ps[:, 2560:2560 + 128:2], ACT.Sign, "ps5", "sgb")
     qz(*pair("sq3", "ss3", 0, 128), T.ring[:, 0:512], four("hA%d"), "sA")
     mm(3, VQ, pair("sq3", "ss3", 0, 128), "vq sA", w=128)
     dma("y", "dout", 144, T.oc[:, 0:512], u8(T.sq3[:, 0:128]), "sA", "")
     for b in range(4):
         scaled("vs"[b % 2], T.ring[:, 512 + b:1024:4], second[b], 0.03125, "hB%d" % b, 128)
-    act(T.sg[:], T.ps[:, 512:512 + C:2], ACT.Sign, "ps1", "sg")
+    tt(T.tm[:], T.sg[:], T.hi[:], A.min, "sg sgb hi", "tm")
     qz(*pair("sq3", "ss3", 128, C), T.ring[:, 512:1024], four("hB%d"), "sB")
     mm(4, VQ, pair("sq3", "ss3", 128, C), "vq sB", w=128)
     act(T.yo[:, 0:128], bank(3, 128), ACT.Copy, "ps3", "yA")
@@ -411,11 +422,10 @@ def rank_program(g, core, T, topo):
     dma("y", "dout", 144, T.y[:, 0:128], T.yo[:, 0:128], "yA", "")
     for k in range(4):
         dma("y" if k < 2 else "s", "dout", 144, T.osc[4 * k:4 * k + 4, :], T.ss3[32 * k:32 * k + 4, :], "sA sB", "")
-    tt(T.tm[:], T.sg[:], T.hi[:], A.min, "sg hi", "tm")
+    tt(T.d2[:], T.tm[:], T.lo[:], A.max, "tm lo", "d2")
     act(T.yo[:, 128:256], bank(4, 128), ACT.Copy, "ps4", "yB")
     dma("s", "dout", 144, T.y[:, 128:256], T.yo[:, 128:256], "yB", "")
-    tt(T.d2[:], T.tm[:], T.lo[:], A.max, "tm lo", "d2")
-    tt(T.lf[:, 0:256:2], T.lf[:, 0:256:2], T.d2[:], A.add, "d2 lf", "lf")
+    tt(T.lf[:, 0:256:2], T.d2[:], T.lf[:, 0:256:2], A.subtract, "d2 lf", "lf")
     dma("y", "dout", 144, T.ol[:], T.lf[0:128:16, :], "lf", "")
 
     for s in total:

from concourse.mybir import dt, AluOpType, AxisListType, ActivationFunctionType

C = 256
BIG = 2.0 ** 96
DIRECT = [5, 6, 7, 8, 9]
SIGNED = [c for c in range(16) if c not in DIRECT]

X4, U8, BF, F32, I32, U16 = "float8_e4m3fn_x4", "uint8", "bfloat16", "float32", "int32", "uint16"
SCRATCH = {"ps": ("psum", [128, 4096], F32)}
for _d, _names in (
        (X4, "wq:512 uq:128 uq2:256 vq:128 eq:512 gq:128 zq:256 mq:1280 sq0:256 sq1:256 sq2:256 sq3:256 lq0:256 lq1:256 lq2:256"),
        (U8, "wsc:512 us:128 us2:256 vs:128 es:512 gs:128 zs:256 ms:1280 ss0:256 ss1:256 ss2:256 ss3:256 ls0:256 ls1:256 ls2:256"),
        (U16, "eo1:4 eo2:4 el1:4 el2:4 ulu:16 ownu:64 faru:48 au:16 fu:16 cu:16 llu:64 endu:4"),
        (I32, "ia:16 ib:16 if_:16 im:16 pi:4 bi:32"),
        (BF, "ring:7168 xb:1024 ub:512 vb:512 ones:514 c0:514 c1:514 g8:512 gt:512 y16:256 m0:256 mask2:256 reset:256 keep:256 tb:16 "
             "wv:256 fr:256 e0:256 er0:256 e1:256 er1:256 e2:256 er2:256 hi:128 lo:128 mx:128 mn:128 sg:128 tm:128 d2:128 ym:256 ys:256 "
             "own:1024 z:1024 dpl:1024 bord:1536 mt:5120"),
        (F32, "pf:8 jf:256 nb:8 node2:32 t1:16 t2:16 t3:16 off0:64 off1:64 off2:64 o0:16 dp:16 t5:16 mk:32 mk2:32 mk3:32 t64:16 ac:32 xx:32 "
              "t0:32 ll:64 lf:256 d1:256 sc:256 key:260 junk:1040 junkv:260 ff:8 fd:4 yo:256")):
    for _e in _names.split():
        SCRATCH[_e.split(":")[0]] = ("sbuf", [128, int(_e.split(":")[1])], _d)
SEMAPHORES = ["cv", "cs", "ct", "cg", "sent", "arr0", "arr1", "arr2", "lst1", "lst2",
              "dxb", "dx", "du", "dv", "dw", "dla", "dlb", "dda", "ddb", "dout"]

A = AluOpType
ACT = ActivationFunctionType


def rank_program(g, core, T, topo):
    rank = T.rank_of(core)
    if rank is None:
        return
    n = len(T.cores)
    nxt = T.cores[(rank + 1) % n]
    prv = T.cores[(rank - 1) % n]
    rid, pid, _ = topo.addr(nxt)
    out_eng = topo.engines(core, nxt)[:8]
    mask = sum(1 << e for e in out_eng)
    n_in = len(topo.engines(prv, core)[:8])

    Q = {"g": g, "v": g.vector, "s": g.scalar, "t": g.tensor, "y": g.sync}
    csem = {"g": "cg", "v": "cv", "s": "cs", "t": "ct"}
    total, snap, writer, readers, waited = {}, {}, {}, {}, {}
    known = {q: {} for q in Q}

    def wait(q, ev):
        s, v = ev
        if known[q].get(s, 0) >= v:
            return
        Q[q].wait_ge(T.sem[s], v)
        waited[s] = max(waited.get(s, 0), v)
        known[q][s] = v
        for k, w in snap.get(ev, {}).items():
            if known[q].get(k, 0) < w:
                known[q][k] = w

    def deps(q, reads, writes):
        need = []
        for r in reads:
            if r in writer:
                need.append(writer[r])
            if r.startswith("ps"):
                need += [e for e in readers.get(r, []) if e[0] != csem.get(q)]
        for w in writes:
            if w in writer:
                need.append(writer[w])
            need += readers.get(w, [])
        if q == "t":
            need = [e for e in need if e[0] != "ct"]
        best = {}
        for s, v in need:
            best[s] = max(best.get(s, 0), v)
        for s in sorted(best, key=lambda k: -len(snap.get((k, best[k]), {}))):
            wait(q, (s, best[s]))

    def done(ev, q, reads, writes):
        new = dict(known[q])
        for k, w in snap.get(ev, {}).items():
            new[k] = max(new.get(k, 0), w)
        snap[ev] = new
        for r in reads:
            readers.setdefault(r, []).append(ev)
        for w in writes:
            writer[w] = ev
            readers[w] = []

    def op(q, fn, reads, writes):
        reads, writes = reads.split(), writes.split()
        deps(q, reads, writes)
        s = csem[q]
        total[s] = total.get(s, 0) + 1
        fn().then_inc(T.sem[s], 1)
        done((s, total[s]), q, reads, writes)

    def dma(q, sem, whole, out, in_, reads, writes):
        reads, writes = reads.split(), writes.split()
        deps(q, reads, [])
        Q[q].dma_start(out, in_).then_inc(T.sem[sem], 16)
        total[sem] = whole
        done((sem, whole), q, reads, writes)

    def send(out, in_, sem, reads):
        deps("g", reads.split(), [])
        g.remote_dma(out, in_, T.sem[sem], T.sem.sent, pid, rid, mask)
        total["sent"] = total.get("sent", 0) + len(out_eng)

    V, S, P = g.vector, g.scalar, g.tensor

    def ts(out, in0, s1, o0, reads, writes, s2=None, o1=None):
        if o1 is None:
            op("v", lambda: V.tensor_scalar(out, in0, s1, None, o0), reads, writes)
        else:
            op("v", lambda: V.tensor_scalar(out, in0, s1, s2, o0, o1), reads, writes)

    def tt(out, a, b, o, reads, writes):
        op("v", lambda: V.tensor_tensor(out, a, b, o), reads, writes)

    def cp(out, a, reads, writes):
        op("v", lambda: V.tensor_copy(out, a), reads, writes)

    def qz(q, s, a, reads, writes):
        op("v", lambda: V.quantize_mx(q, s, a), reads, writes)

    def scan(out, d0, d1, o0, o1, reads, writes):
        op("v", lambda: V.tensor_tensor_scan(out, d0, d1, 0.0, o0, o1), reads, writes)

    def act(out, a, f, reads, writes, **kw):
        op("s", lambda: S.activation(out, a, f, **kw), reads, writes)

    def bank(k, w=C):
        return T.ps[:, 512 * k:512 * k + w]

    def pair(q, s, a, b):
        return T[q][:, a:b], T[s][:, a:b]

    def mm(k, l, r, reads, start=True, stop=True, w=C):
        op("t", lambda: P.matmul_mx(bank(k, w), l[0], l[1], r[0], r[1], start, stop), reads, "ps%d" % k)

    def scaled(q, out, k, f, name, w=C):
        if q == "v":
            ts(out, bank(k, w), f, A.mult, "ps%d" % k, name)
        else:
            act(out, bank(k, w), ACT.Copy, "ps%d" % k, name, scale=f)

    def iota(out, pattern, base, cm, name):
        op("g", lambda: g.iota(out, pattern, base, cm, allow_small_or_imprecise_dtypes=True), "", name)

    def u8(b):
        return b.bitcast(dt.uint8)

    def four(s):
        return " ".join(s % b for b in range(4))

    for s, k, w in (("arr0", 2, "l0"), ("arr1", 2, "l1"), ("arr2", 2, "l2"), ("lst1", 1, "el1"), ("lst2", 1, "el2")):
        total[s] = k * n_in
        writer[w] = (s, k * n_in)

    for k in range(4):
        dma("y" if k < 2 else "s", "dxb", 64, T.xb[:, 256 * k:256 * k + 256], T.x[:, 1024 * k:1024 * k + 256], "", "xb")
    dma("y", "dla", 16, T.ia[:], T.la[:], "", "ia")
    dma("s", "dda", 16, T.if_[:], T.da[:], "", "if")
    dma("y", "dlb", 16, T.ib[:], T.lb[:], "", "ib")
    dma("s", "ddb", 16, T.im[:], T.db[:], "", "im")
    dma("s", "du", 16, T.ub[:], T.u[:], "", "ub")
    for k in range(4):
        dma("y", "dx", 64, T.ring[:, 3072 + 1024 * k + 256:4096 + 1024 * k], T.x[:, 1024 * k + 256:1024 * k + 1024], "", "ringx")
    for k in range(4):
        act(T.ring[:, 3072 + 1024 * k:3072 + 1024 * k + 256], T.xb[:, 256 * k:256 * k + 256], ACT.Copy, "xb", "rx%d" % k)

    op("v", lambda: V.memset(T.ones[:], 1.0), "", "ones")
    op("g", lambda: g.iota(T.pi[:, 3:4], [[1, 1]], 0, 1), "", "pi3")
    iota(T.y16[:], [[0, 16], [1, 16]], 0, 0, "y16")
    iota(T.jf[:], [[1, 256]], 0, 0, "jf")
    op("g", lambda: g.affine_select(T.c0[:], T.ones[:], [[1, 514]], A.is_equal, 0.0, -2, -4), "ones", "c0")
    op("v", lambda: V.memset(T.lf[:], 0.0), "", "lf")
    ts(T.pi[:, 0:1], T.pi[:, 3:4], 15, A.bitwise_and, "pi3", "pi0")
    ts(T.pi[:, 1:2], T.pi[:, 3:4], 4, A.logical_shift_right, "pi3", "pi1")
    ts(T.pi[:, 2:3], T.pi[:, 3:4], 1, A.bitwise_and, "pi3", "pi2")
    ts(T.reset[:], T.y16[:], 0.0, A.is_equal, "y16", "reset", BIG, A.mult)
    cp(T.pf[:, 0:3], T.pi[:, 0:3], "pi0 pi1 pi2", "pf")
    ts(T.keep[:], T.y16[:], 0.0, A.not_equal, "y16", "keep")
    R_, G_, PAR, R4, S1024, SINV, PAR4, R16 = [T.pf[:, k:k + 1] for k in range(8)]
    ts(R4, R_, 4.0, A.mult, "pf", "r4")
    ts(S1024, PAR, -2048.0, A.mult, "pf", "s1024", 1024.0, A.add)
    ts(SINV, PAR, -2.0 / 1024, A.mult, "pf", "sinv", 1.0 / 1024, A.add)
    ts(PAR4, PAR, 4.0, A.mult, "pf", "par4")
    ts(R16, R_, 16.0, A.mult, "pf", "r16", 15.0, A.add)
    ts(T.mask2[:], T.y16[:], R_, A.not_equal, "y16 pf", "mask2", BIG, A.mult)
    ts(T.m0[:], T.y16[:], R_, A.is_equal, "y16 pf s1024", "m0", S1024, A.mult)
    ts(T.endu[:], T.y16[:, 0:4], 0.0, A.mult, "y16 r16", "endu", R16, A.add)
    ts(T.nb[:, 0:5], T.jf[:, 1:6], R4, A.add, "jf r4", "nb", -256.0, A.mult)
    ts(T.key[:, 256:260], T.jf[:, 0:4], 257.0, A.add, "jf", "keyx", 256.0, A.mult)
    ts(T.node2[:, 0:16], T.jf[:, 0:256:16], R_, A.add, "jf pf", "node2a")
    ts(T.node2[:, 16:32], T.jf[:, 0:256:16], R_, A.add, "jf pf", "node2b")
    cp(T.ulu[:, 0:8], T.jf[:, 0:128:16], "jf", "ulua")
    cp(T.ulu[:, 8:16], T.jf[:, 1:128:16], "jf", "ulub")

    qz(T.sq0[:], T.ss0[:], T.xb[:], "xb", "s0")
    send(u8(T.lq0[:]), u8(T.sq0[:]), "arr0", "s0")
    send(T.ls0[:], T.ss0[:], "arr0", "s0")
    wait("y", ("sent", total["sent"]))
    dma("y", "dw", 32, u8(T.wq[:]), T.wc[:], "", "w")
    dma("y", "dw", 32, T.wsc[:], T.ws[:], "", "w")
    dma("y", "dv", 16, T.vb[:], T.v[:], "", "vb")
    op("g", lambda: g.affine_select(T.c1[:], T.ones[:], [[1, 514]], A.is_equal, 0.0, -3, -4), "ones", "c1")
    iota(T.tb[:, 0:4], [[1, 4]], 0, 0, "tba")
    iota(T.tb[:, 4:8], [[-1, 4]], 0, 0, "tbb")
    iota(T.g8[:], [[1, 8], [0, 64]], 0, 0, "g8")
    iota(T.mt[:, 4096:5120], [[0, 1024]], 0, 0, "m16")

    def own_gather(t):
        w = (3 - t) * 1024
        act(T.own[:], T.ring[:, w:w + 4096].indirect(T.ownu[:]), ACT.Copy,
            "ringx ownu " + four("rx%d") + "".join(" " + four("h" + str(k) + "_%d") for k in range(t)), "own", scale=0.5)

    cp(T.au[:], T.ia[:], "ia", "au")
    qz(*pair("eq", "es", 0, 128), T.c0[:, 2:514], "c0", "E0")
    qz(*pair("eq", "es", 256, 384), T.c0[:, 0:512], "c0", "E2")
    ts(T.t2[:], T.ia[:], 4.0, A.mult, "ia", "t2")
    ts(T.t1[:], T.if_[:], 1024.0, A.mult, "if", "t1")
    cp(T.wv[:].indirect(T.au[:]), T.jf[:], "au jf", "wv")
    tt(T.t3[:], T.t1[:], T.t2[:], A.add, "t1 t2", "t3")
    ts(T.fu[:], T.if_[:], PAR4, A.add, "if par4", "fu")
    for b in range(4):
        ts(T.off0[:, 16 * b:16 * b + 16], T.t3[:], float(b), A.add, "t3", "off0_%d" % b)
    qz(T.uq[:], T.us[:], T.ub[:], "ub", "uq")
    cp(T.ownu[:], T.off0[:], four("off0_%d"), "ownu off0")
    tt(T.ym[:], T.wv[:], T.m0[:], A.mult, "wv m0", "ym")
    act(T.us2[:], T.us[:].indirect(T.ulu[:]), ACT.Copy, "uq ulua ulub", "us2")
    own_gather(0)
    ts(T.t64[:], T.im[:], 64.0, A.mult, "im", "t64")
    scan(T.ys[:], T.keep[:], T.ym[:], A.mult, A.add, "keep ym", "ys")
    tt(T.o0[:], T.t64[:], T.ib[:], A.add, "t64 ib", "o0")
    cp(T.ac[:, 0:16], T.ia[:], "ia", "aca")
    ts(T.ac[:, 16:32], T.ys[:, 15:256:16], SINV, A.mult, "ys sinv", "acb")
    cp(T.faru[:, 0:16], T.o0[:], "o0", "faru0")
    ts(T.bi[:, 0:16], T.ib[:], 3, A.bitwise_and, "ib", "bia")
    cp(T.cu[:], T.ac[:, 16:32], "acb", "cu")
    ts(T.bi[:, 16:32], T.ib[:], 2, A.logical_shift_right, "ib", "bib")
    tt(T.xx[:], T.ac[:], T.node2[:], A.subtract, "aca acb node2a node2b", "xx")
    ts(T.t5[:], T.bi[:, 0:16], 5.0, A.mult, "bia", "t5")
    cp(T.uq2[:].bitcast(dt.uint32), T.uq[:].bitcast(dt.uint32).indirect(T.ulu[:]), "uq ulua ulub", "uq2")
    qz(*pair("eq", "es", 128, 256), T.c1[:, 2:514], "c1", "E1")
    qz(*pair("eq", "es", 384, 512), T.c1[:, 0:512], "c1", "E3")
    act(T.fr[:], T.tb[:, 0:8].indirect(T.fu[:]), ACT.Copy, "tba tbb fu", "fr")
    act(T.er0[:], T.fr[:].indirect(T.cu[:]), ACT.Copy, "fr cu", "er0")
    ts(T.t0[:], T.xx[:], PAR, A.mult, "xx pf", "t0")
    tt(T.dp[:], T.t5[:], T.bi[:, 16:32], A.subtract, "t5 bib", "dp")
    ts(T.mk[:, 0:16], T.im[:], 1.0, A.is_lt, "im", "mka", 3.0, A.mult)
    ts(T.mk[:, 16:32], T.im[:], 2.0, A.is_lt, "im", "mkb", 3.0, A.mult)
    tt(T.ll[:, 0:32], T.t0[:], T.node2[:], A.add, "t0 node2a node2b", "lla")
    tt(T.ll[:, 32:64], T.ac[:], T.t0[:], A.subtract, "t0 aca acb", "llb")
    tt(T.mk2[:, 0:16], T.mk[:, 0:16], T.dp[:], A.mult, "mka dp", "mk2a")
    tt(T.mk2[:, 16:32], T.mk[:, 16:32], T.dp[:], A.mult, "mkb dp", "mk2b")
    cp(T.llu[:], T.ll[:], "lla llb", "llu")
    tt(T.mk3[:, 0:16], T.mk2[:, 0:16], T.o0[:], A.add, "mk2a o0", "mk3a")
    tt(T.mk3[:, 16:32], T.mk2[:, 16:32], T.o0[:], A.add, "mk2b o0", "mk3b")
    ts(T.gt[:], T.g8[:], G_, A.is_equal, "g8 pf", "gt", 256.0, A.mult)
    cp(T.faru[:, 16:48], T.mk3[:], "mk3a mk3b", "faru1 faru2")
    qz(T.gq[:], T.gs[:], T.gt[:], "gt", "gq")

    def unpack(t):
        for b in range(4):
            mm(2 + b, pair("eq", "es", 128 * b, 128 * b + 128), pair("lq%d" % t, "ls%d" % t, 0, C), "E%d l%d" % (b, t))

    unpack(0)
    for b in range(4):
        scaled("v" if b == 0 else "s", T.bord[:, 384 * b + 128:384 * b + 384], 2 + b, 0.5, "bx%d" % b)

    slots = DIRECT + SIGNED
    UO, UL, ZT = pair("uq2", "us2", 0, 128), pair("uq2", "us2", 128, 256), pair("zq", "zs", 0, C)

    def wb(b):
        return pair("wq", "wsc", 128 * b, 128 * b + 128)

    def row(c, a, b):
        s = slots.index(c)
        base = 1024 * (s // 4) + s % 4
        return T.mt[:, base + 4 * a:base + 4 * (b - 1) + 1:4]

    def sum_tile(k, first, last):
        names = "m16" if k == 4 else " ".join("m%d%s" % (slots[4 * k + i], h) for i in range(4) for h in "ab")
        m = pair("mq", "ms", 256 * k, 256 * k + 256)
        qz(*m, T.mt[:, 1024 * k:1024 * k + 1024], names, "mq%d" % k)
        mm(6, pair("gq", "gs", 0, 128), m, "gq mq%d" % k, first, last)

    def picked(t):
        for b in range(4):
            o = T.bord[:, 384 * b + 64 * (2 - t):384 * b + 64 * (3 - t)]
            w = T.dpl[:, 256 * b:256 * b + 256].indirect(T["el%d" % t][:])
            rd, wr = "dpl%d el%d" % (b, t), "b%d_%d" % (t, b)
            if b == 0:
                cp(o, w, rd, wr)
            else:
                act(o, w, ACT.Copy, rd, wr)

    def reading(t, a, e, name):
        for b in range(4):
            w0 = 384 * b + 64 * (2 - t)
            tt(T.z[:, 4 * a + b:4 * e:4], T.bord[:, w0:w0 + 256].indirect(T.faru[:, 16 * t + a // 16:16 * t + e // 16]),
               T.own[:, 256 * b + a:256 * b + e], A.add,
               "bx%d own faru%d " % (b, t) + " ".join("b%d_%d" % (k, b) for k in range(1, t + 1)), "z%d%s" % (b, name[0]))
        qz(*pair("zq", "zs", a, e), T.z[:, 4 * a:4 * e], four("z%d" + name[0]), " ".join("zq" + h for h in name))

    for t in range(2):
        if t > 0:
            picked(t)
        reading(t, 0, C, "AB")
        mm(0, UO, ZT, "uq2 us2 zqA")
        for b in range(4):
            mm(2 + b, wb(b), ZT, "w zqA")
        mm(7, UO, ZT, "uq2 us2 zqA")
        mm(1, UL, ZT, "uq2 us2 zqA zqB")
        h0 = (2 - t) * 1024
        sq, ss, u = T["sq%d" % (t + 1)], T["ss%d" % (t + 1)], t + 1
        if t == 0:
            act(T.e0[:, 0:256:2], T.fr[:, 0:256:2], ACT.Identity, "fr", "e0a", bias=-3.0)
            act(T.e0[:, 1:256:2], T.fr[:, 1:256:2], ACT.Identity, "fr", "e0b", bias=3.0)
        for b in range(4):
            scaled("s", T.ring[:, h0 + b:h0 + 1024:4], 2 + b, 0.03125, "h%d_%d" % (t, b))
        act(T.sg[:], T.ps[:, 512 + t:512 + C:2], ACT.Sign, "ps1", "sg", scale=-1.0 if t == 0 else 1.0)

        if t == 0:
            tt(T.hi[:], T.e0[:, 0:256:2], T.er0[:, 0:256:2], A.max, "e0a er0", "hi")
        tt(T.d1[:], bank(0), T.mask2[:], A.add, "ps0 mask2", "d1")
        if t == 0:
            tt(T.mn[:], T.e0[:, 0:256:2], T.er0[:, 0:256:2], A.min, "e0a er0", "mn")
        scan(T.sc[:], T.reset[:], T.d1[:], A.add, A.min, "reset d1", "sc")
        if t == 0:
            ts(T.lo[:], T.mn[:], 3.0, A.add, "mn", "lo")
        tt(T.mt[:, 4096:5120:4], bank(0), T.sc[:], A.is_equal, "ps0 sc", "m16")
        for c in SIGNED:
            act(row(c, 0, C), bank(7), ACT.Sign, "ps7 sc", "m%da m%db" % (c, c), bias=T.sc[:, 16 * c + 15:16 * c + 16], scale=-1.0)
        for i, c in enumerate(DIRECT):
            e = 16 * c + 16
            col = T.sc[:, e - 1:e]
            ts(row(c, 0, e), T.ps[:, 0:e], col, A.is_lt, "ps0 sc", "m%da" % c)
            if e < C:
                ts(row(c, e, C), T.ps[:, e:C], col, A.is_le, "ps0 sc", "m%db" % c)
            if i == 0:
                sum_tile(4, True, False)
            if i == 2:
                qz(sq[:], ss[:], T.ring[:, h0:h0 + 1024], four("h" + str(t) + "_%d"), "s%d" % u)
                send(u8(T["lq%d" % u][:]), u8(sq[:]), "arr%d" % u, "s%d" % u)
                send(T["ls%d" % u][:], ss[:], "arr%d" % u, "s%d" % u)
        for k in range(len(DIRECT) // 4):
            sum_tile(k, False, False)
        pend = []
        for c in SIGNED:
            e = 16 * c + 16
            ts(row(c, 0, e), row(c, 0, e), 0.0, A.is_gt, "m%da" % c, "m%da" % c)
            if e < C:
                ts(row(c, e, C), row(c, e, C), 0.0, A.is_ge, "m%db" % c, "m%db" % c)
            for k in pend:
                sum_tile(k, False, False)
            s = slots.index(c)
            pend = [s // 4] if s % 4 == 3 else []
        sum_tile(3, False, True)
        tt(T.tm[:], T.sg[:], T.hi[:], A.max if t == 0 else A.min, "sg hi", "tm")
        tt(T.key[:, 0:C], bank(6), T.jf[:], A.add, "ps6 jf", "key")
        for c in range(4):
            act(T.junk[:, 260 * c:260 * c + C + c], T.key[:, 0:C + c], ACT.Relu, "key keyx nb", "junk%d ff%d" % (c, c),
                bias=T.nb[:, c:c + 1], accum_out=T.ff[:, c:c + 1])
        la_, lc_ = T.llu[:, 32 * t:32 * t + 16], T.llu[:, 32 * t + 16:32 * t + 32]
        tt(T.lf[:, t:256:2], T.tm[:], T.lo[:], A.min if t == 0 else A.max, "tm lo", "lf")
        ts(T.junkv[:], T.key[:], T.nb[:, 4:5], A.add, "key keyx nb", "junk4", 0.0, A.max)
        tt(T.ym[:], T.lf[:].indirect(la_), T.m0[:], A.mult, "lf llu m0", "ym")
        op("v", lambda: V.tensor_reduce(T.ff[:, 4:5], T.junkv[:], AxisListType.X, A.add), "junk4", "ff4")
        scan(T.ys[:], T.keep[:], T.ym[:], A.mult, A.subtract, "keep ym", "ys")
        tt(T.fd[:], T.ff[:, 0:4], T.ff[:, 1:5], A.subtract, "ff4 " + four("ff%d"), "fd")
        tt(T["off%d" % u][:], T.ys[:].indirect(T.endu[:]), T["off%d" % t][:], A.add, "ys endu off%d" % t, "off%d" % u)
        cp(T["eo%d" % u][:], T.fd[:], "fd", "eo%d" % u)
        send(T["el%d" % u][:], T["eo%d" % u][:], "lst%d" % u, "eo%d" % u)

        unpack(u)
        cp(T.ownu[:], T["off%d" % u][:], "off%d" % u, "ownu")
        own_gather(u)
        for b in range(4):
            scaled("v" if b < 2 else "s", T.dpl[:, 256 * b:256 * b + 256], 2 + b, 0.5, "dpl%d" % b)
        if t == 0:
            tt(T.e1[:], T.lf[:].indirect(la_), T.e0[:], A.subtract, "lf llu e0a e0b", "e1")
            tt(T.er1[:], T.lf[:].indirect(lc_), T.er0[:], A.subtract, "lf llu er0", "er1")
            a_, b_ = T.e1[:, 1:256:2], T.er1[:, 1:256:2]
            tt(T.mx[:], a_, b_, A.max, "e1 er1", "mx")
            tt(T.mn[:], a_, b_, A.min, "e1 er1", "mn")
            ts(T.hi[:], T.mx[:], -1.0, A.mult, "mx", "hi")
            ts(T.lo[:], T.mn[:], -1.0, A.mult, "mn", "lo", -3.0, A.add)
        else:
            tt(T.e2[:], T.lf[:].indirect(la_), T.e1[:], A.add, "lf llu e1", "e2")
            tt(T.er2[:], T.lf[:].indirect(lc_), T.er1[:], A.add, "lf llu er1", "er2")
            a_, b_ = T.e2[:, 0:256:2], T.er2[:, 0:256:2]
            tt(T.mx[:], a_, b_, A.max, "e2 er2", "mx")
            tt(T.hi[:], a_, b_, A.min, "e2 er2", "hi")
            ts(T.lo[:], T.mx[:], -3.0, A.add, "mx", "lo")
            qz(T.vq[:], T.vs[:], T.vb[:], "vb", "vq")

    picked(2)
    VQ = pair("vq", "vs", 0, 128)
    ZA, ZB = pair("zq", "zs", 0, 128), pair("zq", "zs", 128, C)
    reading(2, 0, 128, "A")
    for b in range(4):
        mm(2 + b, wb(b), ZA, "w zqA", w=128)
        scaled("s", T.ring[:, b:512:4], 2 + b, 0.03125, "hA%d" % b, 128)
    mm(1, UL, ZA, "uq2 us2 zqA", w=128)
    act(T.sg[:, 0:64], T.ps[:, 512:512 + 128:2], ACT.Sign, "ps1", "sg")
    reading(2, 128, C, "B")
    second = (0, 6, 7, 2)
    mm(5, UL, ZB, "uq2 us2 zqB", w=128)
    for b in range(4):
        mm(second[b], wb(b), ZB, "w zqB", w=128)
    act(T.sg[:, 64:128], T.ps[:, 2560:2560 + 128:2], ACT.Sign, "ps5", "sgb")
    qz(*pair("sq3", "ss3", 0, 128), T.ring[:, 0:512], four("hA%d"), "sA")
    mm(3, VQ, pair("sq3", "ss3", 0, 128), "vq sA", w=128)
    dma("y", "dout", 144, T.oc[:, 0:512], u8(T.sq3[:, 0:128]), "sA", "")
    for b in range(4):
        scaled("vs"[b % 2], T.ring[:, 512 + b:1024:4], second[b], 0.03125, "hB%d" % b, 128)
    tt(T.tm[:], T.sg[:], T.hi[:], A.min, "sg sgb hi", "tm")
    qz(*pair("sq3", "ss3", 128, C), T.ring[:, 512:1024], four("hB%d"), "sB")
    mm(4, VQ, pair("sq3", "ss3", 128, C), "vq sB", w=128)
    act(T.yo[:, 0:128], bank(3, 128), ACT.Copy, "ps3", "yA")
    dma("y", "dout", 144, T.oc[:, 512:1024], u8(T.sq3[:, 128:256]), "sB", "")
    dma("y", "dout", 144, T.y[:, 0:128], T.yo[:, 0:128], "yA", "")
    for k in range(4):
        dma("y" if k < 2 else "s", "dout", 144, T.osc[4 * k:4 * k + 4, :], T.ss3[32 * k:32 * k + 4, :], "sA sB", "")
    tt(T.d2[:], T.tm[:], T.lo[:], A.max, "tm lo", "d2")
    act(T.yo[:, 128:256], bank(4, 128), ACT.Copy, "ps4", "yB")
    dma("s", "dout", 144, T.y[:, 128:256], T.yo[:, 128:256], "yB", "")
    tt(T.lf[:, 0:256:2], T.d2[:], T.lf[:, 0:256:2], A.subtract, "d2 lf", "lf")
    dma("y", "dout", 144, T.ol[:], T.lf[0:128:16, :], "lf", "")

    for s in total:
        if waited.get(s, 0) < total[s]:
            wait("g", (s, total[s]))
